import numpy as np
import ml_dtypes

BF16 = ml_dtypes.bfloat16


def bf(x):
    return np.asarray(x, np.float32).astype(BF16)


def f32(x):
    return np.asarray(x, np.float32)


def f64(x):
    return np.asarray(x).astype(np.float64)


def striped(idx):
    return np.tile(idx.reshape(-1, 16).T, (8, 1))


S, K, M, N, V, D, R, H = 512, 128, 256, 320, 192, 3, 64, 128


def sigmoid(v):
    return 1.0 / (1.0 + np.exp(-v))


def setup_inputs():
    return {"table": bf(np.random.standard_normal((K, S))), "w": bf(np.random.standard_normal((D, K, M)) / np.sqrt(D * K)), "b": f32(0.5 * np.random.standard_normal((M, 1))), "offs": striped(np.random.permutation(S)[:N])}


def reference(table, w, b, offs):
    idx = offs[:16].T.reshape(-1)
    x = f64(table)[:, idx]
    y = sum(f64(w)[t].T @ x[:, t * R : t * R + V] for t in range(D))
    y = y + f64(b)
    return np.tanh(y[:H]) * sigmoid(y[H:])

@@ -1,0 +1,55 @@
+import concourse.mybir as mybir
+
+BF16, F32, U16 = mybir.dt.bfloat16, mybir.dt.float32, mybir.dt.uint16
+ACT = mybir.ActivationFunctionType
+
+FLOPS = 2 * 3 * 128 * 256 * 192
+
+TAP_DISTANCE = 64
+ENTRIES_PER_COLUMN = 16
+
+
+def tile_rows_curve_wave_sub_kernel(tc, table, w, b, offs, out):
+    nc = tc.nc
+    features, points = table.shape
+    taps, channels = w.shape[0], w.shape[2]
+    half, outputs = out.shape
+
+    with (
+        tc.tile_pool(name="sbuf", bufs=1) as sbuf,
+        tc.psum_pool(name="psum", bufs=1) as psum,
+    ):
+        offsets = sbuf.tile(list(offs.shape), U16, name="offsets")
+        table_tile = sbuf.tile([features, points], BF16, name="table_tile")
+        weights = sbuf.tile([features, taps, channels], BF16, name="weights")
+        bias = sbuf.tile([half, 2], F32, name="bias")
+
+        nc.sync.dma_start(offsets[:], offs)
+        nc.sync.dma_start(table_tile[:], table)
+        nc.scalar.dma_start(weights[:], w.rearrange("t k m -> k t m"))
+        nc.scalar.dma_start(bias[:], b.rearrange("(a p) o -> p (a o)", p=half))
+
+        def convolve(bank, first_channel):
+            for t in range(taps):
+                first = t * TAP_DISTANCE // ENTRIES_PER_COLUMN
+                picked = table_tile[:].indirect(offsets[:, first : first + outputs // ENTRIES_PER_COLUMN])
+                nc.tensor.matmul(
+                    bank[:],
+                    weights[:, t, first_channel : first_channel + half],
+                    picked,
+                    start=(t == 0),
+                    stop=(t == taps - 1),
+                )
+
+        gate_sum = psum.tile([half, outputs], F32, name="gate_sum")
+        filter_sum = psum.tile([half, outputs], F32, name="filter_sum")
+        gate = sbuf.tile([half, outputs], F32, name="gate")
+        filtered = sbuf.tile([half, outputs], F32, name="filtered")
+        result = sbuf.tile([half, outputs], F32, name="result")
+
+        convolve(gate_sum, half)
+        nc.scalar.activation(gate[:], gate_sum[:], ACT.Sigmoid, bias=bias[:, 1:2])
+        convolve(filter_sum, 0)
+        nc.scalar.activation(filtered[:], filter_sum[:], ACT.Tanh, bias=bias[:, 0:1])
+        nc.vector.tensor_tensor(result[:], filtered[:], gate[:], mybir.AluOpType.mult)
+        nc.sync.dma_start(out, result[:])

@@ -29,6 +29,11 @@ def tile_rows_curve_wave_sub_kernel(tc, table, w, b, offs, out):
         nc.scalar.dma_start(weights[:], w.rearrange("t k m -> k t m"))
         nc.scalar.dma_start(bias[:], b.rearrange("(a p) o -> p (a o)", p=half))
 
+        warm_in = sbuf.tile([half, 1], F32, name="warm_in")
+        warm_out = sbuf.tile([half, 1], F32, name="warm_out")
+        nc.vector.memset(warm_in[:], 0.0)
+        nc.scalar.activation(warm_out[:], warm_in[:], ACT.Sigmoid)
+
         def convolve(bank, first_channel):
             for t in range(taps):
                 first = t * TAP_DISTANCE // ENTRIES_PER_COLUMN

@@ -24,20 +24,27 @@ def tile_rows_curve_wave_sub_kernel(tc, table, w, b, offs, out):
         weights = sbuf.tile([features, taps, channels], BF16, name="weights")
         bias = sbuf.tile([half, 2], F32, name="bias")
 
-        nc.sync.dma_start(offsets[:], offs)
         nc.sync.dma_start(table_tile[:], table)
-        nc.scalar.dma_start(weights[:], w.rearrange("t k m -> k t m"))
-        nc.scalar.dma_start(bias[:], b.rearrange("(a p) o -> p (a o)", p=half))
+        nc.scalar.dma_start(weights[:, 0, :], w[0])
+        nc.sync.dma_start(offsets[:], offs)
+        nc.sync.dma_start(weights[:, 1:, :], w[1:].rearrange("t k m -> k t m"))
+        nc.sync.dma_start(bias[:], b.rearrange("(a p) o -> p (a o)", p=half))
 
         warm_in = sbuf.tile([half, 1], F32, name="warm_in")
         warm_out = sbuf.tile([half, 1], F32, name="warm_out")
         nc.vector.memset(warm_in[:], 0.0)
         nc.scalar.activation(warm_out[:], warm_in[:], ACT.Sigmoid)
 
-        def convolve(bank, first_channel):
-            for t in range(taps):
-                first = t * TAP_DISTANCE // ENTRIES_PER_COLUMN
-                picked = table_tile[:].indirect(offsets[:, first : first + outputs // ENTRIES_PER_COLUMN])
+        gate_sum = psum.tile([half, outputs], F32, name="gate_sum")
+        filter_sum = psum.tile([half, outputs], F32, name="filter_sum")
+        gate = sbuf.tile([half, outputs], F32, name="gate")
+        filtered = sbuf.tile([half, outputs], F32, name="filtered")
+        result = sbuf.tile([half, outputs], F32, name="result")
+
+        for t in range(taps):
+            first = t * TAP_DISTANCE // ENTRIES_PER_COLUMN
+            picked = table_tile[:].indirect(offsets[:, first : first + outputs // ENTRIES_PER_COLUMN])
+            for bank, first_channel in ((gate_sum, half), (filter_sum, 0)):
                 nc.tensor.matmul(
                     bank[:],
                     weights[:, t, first_channel : first_channel + half],
@@ -46,15 +53,7 @@ def tile_rows_curve_wave_sub_kernel(tc, table, w, b, offs, out):
                     stop=(t == taps - 1),
                 )
 
-        gate_sum = psum.tile([half, outputs], F32, name="gate_sum")
-        filter_sum = psum.tile([half, outputs], F32, name="filter_sum")
-        gate = sbuf.tile([half, outputs], F32, name="gate")
-        filtered = sbuf.tile([half, outputs], F32, name="filtered")
-        result = sbuf.tile([half, outputs], F32, name="result")
-
-        convolve(gate_sum, half)
         nc.scalar.activation(gate[:], gate_sum[:], ACT.Sigmoid, bias=bias[:, 1:2])
-        convolve(filter_sum, 0)
         nc.scalar.activation(filtered[:], filter_sum[:], ACT.Tanh, bias=bias[:, 0:1])
         nc.vector.tensor_tensor(result[:], filtered[:], gate[:], mybir.AluOpType.mult)
         nc.sync.dma_start(out, result[:])

@@ -7,6 +7,7 @@ FLOPS = 2 * 3 * 128 * 256 * 192
 
 TAP_DISTANCE = 64
 ENTRIES_PER_COLUMN = 16
+LAST_PIECE = 64
 
 
 def tile_rows_curve_wave_sub_kernel(tc, table, w, b, offs, out):
@@ -35,25 +36,34 @@ def tile_rows_curve_wave_sub_kernel(tc, table, w, b, offs, out):
         nc.vector.memset(warm_in[:], 0.0)
         nc.scalar.activation(warm_out[:], warm_in[:], ACT.Sigmoid)
 
+        pieces = (slice(0, outputs - LAST_PIECE), slice(outputs - LAST_PIECE, outputs))
         gate_sum = psum.tile([half, outputs], F32, name="gate_sum")
-        filter_sum = psum.tile([half, outputs], F32, name="filter_sum")
+        filter_sums = [psum.tile([half, c.stop - c.start], F32, name=f"filter_sum_{c.start}") for c in pieces]
         gate = sbuf.tile([half, outputs], F32, name="gate")
         filtered = sbuf.tile([half, outputs], F32, name="filtered")
         result = sbuf.tile([half, outputs], F32, name="result")
 
-        for t in range(taps):
-            first = t * TAP_DISTANCE // ENTRIES_PER_COLUMN
-            picked = table_tile[:].indirect(offsets[:, first : first + outputs // ENTRIES_PER_COLUMN])
-            for bank, first_channel in ((gate_sum, half), (filter_sum, 0)):
-                nc.tensor.matmul(
-                    bank[:],
-                    weights[:, t, first_channel : first_channel + half],
-                    picked,
-                    start=(t == 0),
-                    stop=(t == taps - 1),
-                )
+        def add_tap(bank, first_channel, columns, t):
+            first = (t * TAP_DISTANCE + columns.start) // ENTRIES_PER_COLUMN
+            last = (t * TAP_DISTANCE + columns.stop) // ENTRIES_PER_COLUMN
+            nc.tensor.matmul(
+                bank[:],
+                weights[:, t, first_channel : first_channel + half],
+                table_tile[:].indirect(offsets[:, first:last]),
+                start=(t == 0),
+                stop=(t == taps - 1),
+            )
 
+        add_tap(gate_sum, half, slice(0, outputs), 0)
+        add_tap(filter_sums[0], 0, pieces[0], 0)
+        add_tap(filter_sums[1], 0, pieces[1], 0)
+        for t in range(1, taps):
+            add_tap(gate_sum, half, slice(0, outputs), t)
         nc.scalar.activation(gate[:], gate_sum[:], ACT.Sigmoid, bias=bias[:, 1:2])
-        nc.scalar.activation(filtered[:], filter_sum[:], ACT.Tanh, bias=bias[:, 0:1])
-        nc.vector.tensor_tensor(result[:], filtered[:], gate[:], mybir.AluOpType.mult)
-        nc.sync.dma_start(out, result[:])
+
+        for filter_sum, columns in zip(filter_sums, pieces):
+            for t in range(1, taps):
+                add_tap(filter_sum, 0, columns, t)
+            nc.scalar.activation(filtered[:, columns], filter_sum[:], ACT.Tanh, bias=bias[:, 0:1])
+            nc.vector.tensor_tensor(result[:, columns], filtered[:, columns], gate[:, columns], mybir.AluOpType.mult)
+            nc.sync.dma_start(out[:, columns], result[:, columns])

import concourse.mybir as mybir

BF16, F32, U16 = mybir.dt.bfloat16, mybir.dt.float32, mybir.dt.uint16
ACT = mybir.ActivationFunctionType

FLOPS = 2 * 3 * 128 * 256 * 192

TAP_DISTANCE = 64
ENTRIES_PER_COLUMN = 16
LAST_PIECE = 64


def tile_rows_curve_wave_sub_kernel(tc, table, w, b, offs, out):
    nc = tc.nc
    features, points = table.shape
    taps, channels = w.shape[0], w.shape[2]
    half, outputs = out.shape

    with (
        tc.tile_pool(name="sbuf", bufs=1) as sbuf,
        tc.psum_pool(name="psum", bufs=1) as psum,
    ):
        offsets = sbuf.tile(list(offs.shape), U16, name="offsets")
        table_tile = sbuf.tile([features, points], BF16, name="table_tile")
        weights = sbuf.tile([features, taps, channels], BF16, name="weights")
        bias = sbuf.tile([half, 2], F32, name="bias")

        nc.sync.dma_start(table_tile[:], table)
        nc.scalar.dma_start(weights[:, 0, :], w[0])
        nc.sync.dma_start(offsets[:], offs)
        nc.sync.dma_start(weights[:, 1:, :], w[1:].rearrange("t k m -> k t m"))
        nc.sync.dma_start(bias[:], b.rearrange("(a p) o -> p (a o)", p=half))

        warm_in = sbuf.tile([half, 1], F32, name="warm_in")
        warm_out = sbuf.tile([half, 1], F32, name="warm_out")
        nc.vector.memset(warm_in[:], 0.0)
        nc.scalar.activation(warm_out[:], warm_in[:], ACT.Sigmoid)

        pieces = (slice(0, outputs - LAST_PIECE), slice(outputs - LAST_PIECE, outputs))
        gate_sum = psum.tile([half, outputs], F32, name="gate_sum")
        filter_sums = [psum.tile([half, c.stop - c.start], F32, name=f"filter_sum_{c.start}") for c in pieces]
        gate = sbuf.tile([half, outputs], F32, name="gate")
        filtered = sbuf.tile([half, outputs], F32, name="filtered")
        result = sbuf.tile([half, outputs], F32, name="result")

        def add_tap(bank, first_channel, columns, t):
            first = (t * TAP_DISTANCE + columns.start) // ENTRIES_PER_COLUMN
            last = (t * TAP_DISTANCE + columns.stop) // ENTRIES_PER_COLUMN
            nc.tensor.matmul(
                bank[:],
                weights[:, t, first_channel : first_channel + half],
                table_tile[:].indirect(offsets[:, first:last]),
                start=(t == 0),
                stop=(t == taps - 1),
            )

        add_tap(gate_sum, half, slice(0, outputs), 0)
        add_tap(filter_sums[0], 0, pieces[0], 0)
        add_tap(filter_sums[1], 0, pieces[1], 0)
        for t in range(1, taps):
            add_tap(gate_sum, half, slice(0, outputs), t)
        nc.scalar.activation(gate[:], gate_sum[:], ACT.Sigmoid, bias=bias[:, 1:2])

        for filter_sum, columns in zip(filter_sums, pieces):
            for t in range(1, taps):
                add_tap(filter_sum, 0, columns, t)
            nc.scalar.activation(filtered[:, columns], filter_sum[:], ACT.Tanh, bias=bias[:, 0:1])
            nc.vector.tensor_tensor(result[:, columns], filtered[:, columns], gate[:, columns], mybir.AluOpType.mult)
            nc.sync.dma_start(out[:, columns], result[:, columns])
